import numpy as np
import ml_dtypes


def mxq(x, axis, fmt="e4m3"):
    dtype, down = {"e4m3": (ml_dtypes.float8_e4m3fn, 7), "e5m2": (ml_dtypes.float8_e5m2, 14)}[fmt]
    v = np.moveaxis(np.asarray(x, np.float32).astype(ml_dtypes.bfloat16).astype(np.float64), axis, -1)
    blocks = v.reshape(v.shape[:-1] + (-1, 32))
    amax = np.abs(blocks).max(-1, keepdims=True)
    byte = np.maximum(np.where(amax > 0, np.frexp(amax)[1] - 1 + 127, 0) - down, 1)
    scale = np.exp2(byte - 127.0)
    codes = (blocks / scale).astype(np.float32).astype(dtype).astype(np.float64)
    return np.moveaxis((codes * scale).reshape(v.shape), -1, axis)


WIDE = False


def mx_kscale(k):
    if not WIDE:
        return np.ones(k)
    levels = np.array([10, -10, 5, -5, 0])
    if k % 512:
        return np.exp2(np.random.permutation(np.resize(levels, k // 32))).repeat(32)
    a = np.empty((k // 512, 16))
    for p in range(k // 512):
        a[p, :8] = np.random.permutation(np.resize(levels, 8))
        for g in range(8):
            far = levels[np.abs(levels - a[p, g]) >= 10]
            a[p, g + 8] = far[np.random.randint(len(far))]
    return np.exp2(a.ravel()).repeat(32)


def f64(x):
    return np.asarray(x).astype(np.float64)


def striped(idx):
    return np.tile(idx.reshape(-1, 16).T, (8, 1)).astype(np.uint16)


def unstriped(offs):
    return offs[:16].T.reshape(-1).astype(np.int64)


E2M1 = np.array([0.0, 0.5, 1.0, 1.5, 2.0, 3.0, 4.0, 6.0, -0.0, -0.5, -1.0, -1.5, -2.0, -3.0, -4.0, -6.0])


def pack_weight(w, fmt):
    k, n = w.shape
    w = f64(np.asarray(w, np.float32).astype(ml_dtypes.bfloat16)).reshape(k // 32, 32, n)
    amax = np.abs(w).max(1)
    if fmt == "e4m3":
        byte = np.frexp(amax)[1] - 1 + 127 - 7
    else:
        mant, ex = np.frexp(amax / 6.0)
        byte = np.where(mant > 0.5, ex, ex - 1) + 127
    byte = np.clip(np.where(amax > 0, byte, 1), 1, 254)
    scaled = (w * np.exp2(127.0 - byte)[:, None, :]).reshape(k, n).astype(np.float32)
    by_word = np.ascontiguousarray(scaled.reshape(k // 512, 128, 4, n).transpose(0, 1, 3, 2))
    if fmt == "e4m3":
        words = by_word.astype(ml_dtypes.float8_e4m3fn).view(np.uint8)
    else:
        c = by_word.astype(ml_dtypes.float4_e2m1fn).view(np.uint8) & 0xF
        words = (c[..., 0::2] | (c[..., 1::2] << 4)).reshape(k // 512, 128, 2 * n)
    return np.ascontiguousarray(words), np.ascontiguousarray(byte.astype(np.uint8).reshape(k // 512, 16, n))


def unpack_weight(words, scales, fmt):
    g, _, n = scales.shape
    words = np.ascontiguousarray(words).reshape(g, 128, n, -1)
    if fmt == "e4m3":
        vals = words.view(ml_dtypes.float8_e4m3fn).astype(np.float64)
    else:
        nib = np.empty((g, 128, n, 4), np.uint8)
        nib[..., 0::2] = words & 0xF
        nib[..., 1::2] = words >> 4
        vals = E2M1[nib]
    vals = vals * np.repeat(np.exp2(scales.astype(np.float64) - 127.0), 8, axis=1)[..., None]
    return vals.transpose(0, 1, 3, 2).reshape(g * 512, n)


def gelu(v):
    return 0.5 * v * (1.0 + np.tanh(np.sqrt(2.0 / np.pi) * (v + 0.044715 * v**3)))


K, T, S, H, P, N = 1024, 2048, 1024, 512, 512, 512

def setup_inputs():
    n = np.random.standard_normal
    s = mx_kscale(K)[:, None]
    u = mx_kscale(H)[:, None]
    tab_words, tab_scales = pack_weight(n((K, T)) * s, "e4m3")
    w1_words, w1_scales = pack_weight(0.9 * n((K, H)) / np.sqrt(K) / s, "e2m1")
    w2 = 0.9 * n((K, H)) / np.sqrt(K) / s
    w3 = 0.8 * n((K, H)) / np.sqrt(K) / s
    w4_words, w4_scales = pack_weight(1.4 * n((H, N)) / np.sqrt(H) / u, "e4m3")
    lead = np.random.choice([-1.0, 1.0], H) * np.random.uniform(10.0, 30.0, H) * u[:, 0]
    return {
        "tab_words": tab_words, "tab_scales": tab_scales,
        "offs": striped(np.random.permutation(T)[:S]),
        "pos1": striped(np.random.permutation(S)[:P]),
        "pos2": striped(np.random.permutation(S)[:P]),
        "w1_words": w1_words, "w1_scales": w1_scales,
        "w2": w2.astype(np.float32),
        "w3": w3.astype(np.float32),
        "temp": np.random.uniform(0.4, 1.6, H).astype(np.float32),
        "lead": lead.astype(np.float32),
        "tray": (0.4 * n((H, P)) * u).astype(np.float32),
        "w4_words": w4_words, "w4_scales": w4_scales,
    }

def reference(tab_words, tab_scales, offs, pos1, pos2, w1_words, w1_scales, w2, w3,
              temp, lead, tray, w4_words, w4_scales):
    v = unpack_weight(tab_words, tab_scales, "e4m3")[:, unstriped(offs)]
    w1 = unpack_weight(w1_words, w1_scales, "e2m1")
    w4 = unpack_weight(w4_words, w4_scales, "e4m3")
    left = w1.T @ v
    right = mxq(f64(w2), 0, "e4m3").T @ v
    h = np.maximum(left, right)
    g = mxq(f64(w3), 0, "e4m3").T @ v
    top = h.max(axis=1)
    a = np.exp(h[:, unstriped(pos1)] - top[:, None])
    best = g.max(axis=1)
    c = np.exp(f64(temp)[:, None] * (g[:, unstriped(pos2)] - best[:, None]))
    x = a * c * f64(lead)[:, None] + f64(tray)
    return w4.T @ mxq(x, 0, "e4m3")

@@ -1,0 +1,274 @@
+from contextlib import ExitStack
+
+import concourse.mybir as mybir
+
+K, T, S, H, PAIRS, N = 1024, 2048, 1024, 512, 512, 512
+FLOPS = 3 * 2 * K * H * S + 2 * H * N * PAIRS
+
+F32 = mybir.dt.float32
+BF16 = mybir.dt.bfloat16
+I32 = mybir.dt.int32
+U32 = mybir.dt.uint32
+U16 = mybir.dt.uint16
+U8 = mybir.dt.uint8
+FP8X4 = mybir.dt.float8_e4m3fn_x4
+FP4X4 = mybir.dt.float4_e2m1fn_x4
+ALU = mybir.AluOpType
+ACT = mybir.ActivationFunctionType
+AXIS = mybir.AxisListType
+
+P = 128
+PACK = 4
+PASSES = K // (P * PACK)
+QUADS = 4
+BANK = 512
+HALVES = S // BANK
+MH = PAIRS // 2
+
+
+def tile_list_berry_pair_order_kernel(
+    tc, tab_words, tab_scales, offs, pos1, pos2, w1_words, w1_scales, w2, w3, temp, lead, tray, w4_words, w4_scales, out
+):
+    nc = tc.nc
+    with ExitStack() as ctx:
+        lists = ctx.enter_context(tc.tile_pool(name="lists", bufs=1))
+        keep = ctx.enter_context(tc.tile_pool(name="keep", bufs=1))
+        psum = ctx.enter_context(tc.psum_pool(name="psum", bufs=8))
+
+        def held(shape, dtype, name):
+            return keep.tile(shape, dtype, name=name, align_bytes=64)
+
+        offs_sb = lists.tile([P, S // 16], U16, name="offs_sb")
+        pos1_sb = lists.tile([P, PAIRS // 16], U16, name="pos1_sb")
+        pos2_sb = lists.tile([P, PAIRS // 16], U16, name="pos2_sb")
+
+        tab_w = [held([P, T], U32, f"tab_w{a}") for a in range(PASSES)]
+        tab_s = [held([P, T], U8, f"tab_s{a}") for a in range(PASSES)]
+        v_w = [held([P, S], U32, f"v_w{a}") for a in range(PASSES)]
+        v_s = [held([P, S], U8, f"v_s{a}") for a in range(PASSES)]
+        w1_raw = held([P, PASSES * H], U16, "w1_raw")
+        w1_w = held([P, PASSES * H], U16, "w1_w")
+        w1_sraw = held([P, PASSES * H], U8, "w1_sraw")
+        w1_s = held([P, PASSES * H], U8, "w1_s")
+        w4_w = held([P, N], U32, "w4_w")
+        w4_s = held([P, N], U8, "w4_s")
+        temp_sb = held([P, PACK], F32, "temp_sb")
+        ntemp = held([P, PACK], F32, "ntemp")
+        lead_sb = held([P, PACK], F32, "lead_sb")
+        tray_sb = held([P, PACK, PAIRS], F32, "tray_sb")
+        raw = {(w, a): held([P, PACK, H], F32, f"raw{w}{a}") for w in (2, 3) for a in range(PASSES)}
+        rounded = {(w, a): held([P, PACK, P, PACK], BF16, f"rounded{w}{a}") for w in (2, 3) for a in range(PASSES)}
+        codes = {(w, a): held([P, H], U32, f"codes{w}{a}") for w in (2, 3) for a in range(PASSES)}
+        planes = {(w, a): held([P, H], U8, f"planes{w}{a}") for w in (2, 3) for a in range(PASSES)}
+        left = [held([P, S], F32, f"left{i}") for i in range(PACK)]
+        h = [held([P, S], F32, f"h{i}") for i in range(PACK)]
+        g = [held([P, S], F32, f"g{i}") for i in range(PACK)]
+        ntop = held([P, PACK], F32, "ntop")
+        gmax = held([P, PACK * HALVES], F32, "gmax")
+        gbias = held([P, PACK], F32, "gbias")
+        a_look = [held([P, PAIRS], F32, f"a_look{i}") for i in range(PACK)]
+        c_look = [held([P, PAIRS], F32, f"c_look{i}") for i in range(PACK)]
+        c_lead = [held([P, PAIRS], F32, f"c_lead{i}") for i in range(2)]
+        prod = [held([P, PAIRS], F32, f"prod{i}") for i in range(PACK)]
+        x32 = held([P, PACK, PAIRS], F32, "x32")
+        x_bf = [held([P, MH * PACK], BF16, f"x_bf{u}") for u in range(2)]
+        x_w = [held([P, MH], U32, f"x_w{u}") for u in range(2)]
+        x_s = [held([P, MH], U8, f"x_s{u}") for u in range(2)]
+
+        for a in range(PASSES):
+            nc.vector.memset(tab_s[a][:].bitcast(I32), 0)
+        nc.gpsimd.memset(w1_sraw[:].bitcast(I32), 0)
+        nc.gpsimd.memset(w4_s[:].bitcast(I32), 0)
+
+        def load_weight(w, src, a):
+            rows = src[512 * a : 512 * (a + 1), :]
+            nc.sync.dma_start(out=raw[w, a][:], in_=rows.rearrange("(p j) c -> p j c", j=PACK))
+
+        def load_tab_scales(a):
+            for q in range(QUADS):
+                nc.sync.dma_start(
+                    out=tab_s[a][32 * q : 32 * q + 4, :].bitcast(I32),
+                    in_=tab_scales[a, 4 * q : 4 * q + 4, :].bitcast(I32),
+                )
+
+        nc.sync.dma_start(offs_sb[:], offs)
+        nc.sync.dma_start(out=tab_w[0][:].bitcast(I32), in_=tab_words[0].rearrange("p n t -> p (n t)").bitcast(I32))
+        load_tab_scales(0)
+        nc.sync.dma_start(out=tab_w[1][:].bitcast(I32), in_=tab_words[1].rearrange("p n t -> p (n t)").bitcast(I32))
+        load_weight(3, w3, 0)
+        for q in range(QUADS):
+            nc.sync.dma_start(
+                out=w1_sraw[32 * q : 32 * q + 4, :].bitcast(I32).rearrange("r (a n) -> r a n", a=PASSES),
+                in_=w1_scales[:, 4 * q : 4 * q + 4, :].bitcast(I32).rearrange("a r n -> r a n"),
+            )
+        load_weight(3, w3, 1)
+        load_tab_scales(1)
+        nc.sync.dma_start(
+            out=w1_raw[:].bitcast(I32).rearrange("p (a n) -> p a n", a=PASSES),
+            in_=w1_words.bitcast(I32).rearrange("a p n -> p a n"),
+        )
+        load_weight(2, w2, 0)
+        load_weight(2, w2, 1)
+        nc.sync.dma_start(out=temp_sb[:], in_=temp.rearrange("(p i) -> p i", i=PACK))
+        nc.sync.dma_start(pos2_sb[:], pos2)
+        nc.sync.dma_start(pos1_sb[:], pos1)
+        nc.sync.dma_start(out=lead_sb[:], in_=lead.rearrange("(p i) -> p i", i=PACK))
+        nc.sync.dma_start(out=tray_sb[:], in_=tray.rearrange("(p i) m -> p i m", i=PACK))
+        nc.sync.dma_start(out=w4_w[:].bitcast(I32), in_=w4_words[0].rearrange("p n t -> p (n t)").bitcast(I32))
+        for q in range(QUADS):
+            nc.sync.dma_start(
+                out=w4_s[32 * q : 32 * q + 4, :].bitcast(I32), in_=w4_scales[0, 4 * q : 4 * q + 4, :].bitcast(I32)
+            )
+
+        nc.vector.tensor_copy(v_w[0][:], tab_w[0][:].indirect(offs_sb[:]))
+        nc.vector.tensor_copy(v_s[0][:], tab_s[0][:].indirect(offs_sb[:]))
+        nc.vector.tensor_copy(v_w[1][:], tab_w[1][:].indirect(offs_sb[:]))
+
+        nc.gpsimd.tensor_copy(
+            w1_s[:].rearrange("p (a t c e) -> p a c t e", a=PASSES, t=PACK, e=4),
+            w1_sraw[:].rearrange("p (a c e t) -> p a c t e", a=PASSES, t=PACK, e=4),
+        )
+
+        def product(w, i, u):
+            acc = psum.tile([P, BANK], F32, name="acc")
+            cols = slice(BANK * u, BANK * (u + 1))
+            for a in range(PASSES):
+                if w == 1:
+                    lo = H * a + P * i
+                    lhs = w1_w[:, lo : lo + P].bitcast(FP4X4)
+                    lhs_s = w1_s[:, lo : lo + P]
+                else:
+                    lhs = codes[w, a][:, P * i : P * (i + 1)].bitcast(FP8X4)
+                    lhs_s = planes[w, a][:, P * i : P * (i + 1)]
+                nc.tensor.matmul_mx(
+                    out=acc[:], lhsT=lhs, lhsT_scale=lhs_s, rhs=v_w[a][:, cols].bitcast(FP8X4), rhs_scale=v_s[a][:, cols],
+                    start=(a == 0), stop=(a == PASSES - 1),
+                )
+            return acc
+
+        def round_weight(copy, w, a, m0, m1):
+            copy(
+                rounded[w, a][:, :, m0:m1, :].rearrange("p t m j -> p m t j"),
+                raw[w, a][:].rearrange("p j (m t) -> p m t j", t=PACK)[:, m0:m1, :, :],
+            )
+
+        def quantize_weight(w, a):
+            nc.vector.quantize_mx(
+                out=codes[w, a][:].bitcast(FP8X4), scales=planes[w, a][:],
+                in_=rounded[w, a][:].rearrange("p t m j -> p (t m j)"),
+            )
+
+        def g_half(i, u):
+            acc = product(3, i, u)
+            col = HALVES * i + u
+            seed = None if u == 0 else gmax[:, col - 1 : col]
+            nc.vector.tensor_scalar(
+                g[i][:, BANK * u : BANK * (u + 1)], acc[:], 1.0, seed, ALU.mult, ALU.max,
+                accum_out=gmax[:, col : col + 1],
+            )
+
+        def g_look(i):
+            col = HALVES * i + 1
+            nc.scalar.mul(gbias[:, i : i + 1], gmax[:, col : col + 1], ntemp[:, i : i + 1])
+            nc.scalar.activation(
+                c_look[i][:], g[i][:].indirect(pos2_sb[:]), ACT.Exp,
+                bias=gbias[:, i : i + 1], scale=temp_sb[:, i : i + 1],
+            )
+            if i < 2:
+                nc.gpsimd.tensor_scalar(c_lead[i][:], c_look[i][:], lead_sb[:, i : i + 1], 0.0, ALU.mult, ALU.add)
+
+        def left_tile(i):
+            for u in range(HALVES):
+                acc = product(1, i, u)
+                nc.scalar.copy(left[i][:, BANK * u : BANK * (u + 1)], acc[:])
+
+        def h_half(i, u):
+            acc = product(2, i, u)
+            cols = slice(BANK * u, BANK * (u + 1))
+            nc.vector.tensor_tensor(h[i][:, cols], left[i][:, cols], acc[:], ALU.max)
+
+        def h_look(i, pieces):
+            nc.vector.tensor_reduce(ntop[:, i : i + 1], h[i][:], AXIS.X, ALU.max, negate=True)
+            for m0, m1 in pieces:
+                nc.scalar.activation(
+                    a_look[i][:, m0:m1], h[i][:].indirect(pos1_sb[:, m0 // 16 : m1 // 16]), ACT.Exp,
+                    bias=ntop[:, i : i + 1],
+                )
+
+        whole = [(0, PAIRS)]
+        halves = [(0, MH), (MH, PAIRS)]
+
+        def gpsimd_round(dst, src):
+            nc.gpsimd.tensor_scalar(dst, src, 1.0, 0.0, ALU.mult, ALU.add)
+
+        round_weight(nc.scalar.copy, 3, 0, 0, P)
+        quantize_weight(3, 0)
+        round_weight(nc.scalar.copy, 3, 1, 0, P)
+        nc.vector.tensor_copy(v_s[1][:], tab_s[1][:].indirect(offs_sb[:]))
+        quantize_weight(3, 1)
+        nc.scalar.copy(
+            w1_w[:].rearrange("p (a t c e) -> p a c t e", a=PASSES, t=PACK, e=4),
+            w1_raw[:].rearrange("p (a c e t) -> p a c t e", a=PASSES, t=PACK, e=4),
+        )
+        for pair in range(2):
+            for u in range(HALVES):
+                g_half(2 * pair, u)
+                g_half(2 * pair + 1, u)
+        for i in range(PACK):
+            left_tile(i)
+        for a in range(PASSES):
+            round_weight(gpsimd_round, 2, a, 0, P)
+            quantize_weight(2, a)
+        nc.scalar.mul(ntemp[:], temp_sb[:], -1.0)
+        h_half(0, 0)
+        h_half(0, 1)
+        g_look(0)
+        h_half(1, 0)
+        h_look(0, whole)
+        h_half(1, 1)
+        g_look(1)
+        nc.gpsimd.tensor_tensor(prod[0][:], a_look[0][:], c_lead[0][:], ALU.mult)
+        nc.gpsimd.tensor_tensor(x32[:, 0, :], prod[0][:], tray_sb[:, 0, :], ALU.add)
+        h_half(2, 0)
+        h_look(1, whole)
+        h_half(2, 1)
+        g_look(2)
+        nc.gpsimd.tensor_tensor(prod[1][:], a_look[1][:], c_lead[1][:], ALU.mult)
+        nc.gpsimd.tensor_tensor(x32[:, 1, :], prod[1][:], tray_sb[:, 1, :], ALU.add)
+        h_half(3, 0)
+        h_look(2, whole)
+        h_half(3, 1)
+        g_look(3)
+        h_look(3, halves)
+        nc.vector.scalar_tensor_tensor(prod[2][:], a_look[2][:], lead_sb[:, 2:3], c_look[2][:], ALU.mult, ALU.mult)
+        nc.vector.tensor_tensor(x32[:, 2, :], prod[2][:], tray_sb[:, 2, :], ALU.add)
+
+        last = PACK - 1
+        out_view = out.rearrange("(b p) m -> p b m", p=P)
+        for u, (m0, m1) in enumerate(halves):
+            nc.vector.scalar_tensor_tensor(
+                prod[last][:, m0:m1], a_look[last][:, m0:m1], lead_sb[:, last : last + 1], c_look[last][:, m0:m1],
+                ALU.mult, ALU.mult,
+            )
+            nc.vector.tensor_tensor(x32[:, last, m0:m1], prod[last][:, m0:m1], tray_sb[:, last, m0:m1], ALU.add)
+            (nc.vector.tensor_copy, nc.scalar.copy)[u](
+                x_bf[u][:].rearrange("p (c e i) -> p c i e", e=4, i=PACK),
+                x32[:, :, m0:m1].rearrange("p i (c e) -> p c i e", e=4),
+            )
+            nc.vector.quantize_mx(out=x_w[u][:].bitcast(FP8X4), scales=x_s[u][:], in_=x_bf[u][:])
+            for b in range(2):
+                acc = psum.tile([P, BANK], F32, name="acc")
+                for s in range(2):
+                    cols = slice(P * (2 * b + s), P * (2 * b + s + 1))
+                    nc.tensor.matmul_mx(
+                        out=acc[:, MH * s : MH * (s + 1)], lhsT=w4_w[:, cols].bitcast(FP8X4), lhsT_scale=w4_s[:, cols],
+                        rhs=x_w[u][:].bitcast(FP8X4), rhs_scale=x_s[u][:], start=True, stop=True,
+                    )
+                res = held([P, BANK], F32, f"res{u}{b}")
+                if (u + b) % 2 == 0:
+                    nc.vector.tensor_copy(res[:], acc[:])
+                else:
+                    nc.scalar.copy(res[:], acc[:])
+                nc.sync.dma_start(
+                    out=out_view[:, 2 * b : 2 * b + 2, m0:m1], in_=res[:].rearrange("p (s m) -> p s m", s=2)
+                )

@@ -43,9 +43,10 @@ def tile_list_berry_pair_order_kernel(
         pos2_sb = lists.tile([P, PAIRS // 16], U16, name="pos2_sb")
 
         tab_w = [held([P, T], U32, f"tab_w{a}") for a in range(PASSES)]
-        tab_s = [held([P, T], U8, f"tab_s{a}") for a in range(PASSES)]
+        tab_s = held([P, T], U8, "tab_s")
         v_w = [held([P, S], U32, f"v_w{a}") for a in range(PASSES)]
-        v_s = [held([P, S], U8, f"v_s{a}") for a in range(PASSES)]
+        v_s = held([P, S], U8, "v_s")
+        v_s1 = held([P, S], U8, "v_s1")
         w1_raw = held([P, PASSES * H], U16, "w1_raw")
         w1_w = held([P, PASSES * H], U16, "w1_w")
         w1_sraw = held([P, PASSES * H], U8, "w1_sraw")
@@ -57,9 +58,9 @@ def tile_list_berry_pair_order_kernel(
         lead_sb = held([P, PACK], F32, "lead_sb")
         tray_sb = held([P, PACK, PAIRS], F32, "tray_sb")
         raw = {(w, a): held([P, PACK, H], F32, f"raw{w}{a}") for w in (2, 3) for a in range(PASSES)}
-        rounded = {(w, a): held([P, PACK, P, PACK], BF16, f"rounded{w}{a}") for w in (2, 3) for a in range(PASSES)}
-        codes = {(w, a): held([P, H], U32, f"codes{w}{a}") for w in (2, 3) for a in range(PASSES)}
-        planes = {(w, a): held([P, H], U8, f"planes{w}{a}") for w in (2, 3) for a in range(PASSES)}
+        rounded = {w: held([P, PACK, PASSES, P, PACK], BF16, f"rounded{w}") for w in (2, 3)}
+        codes = {(w, b): held([P, 2 * PASSES * P], U32, f"codes{w}{b}") for w in (2, 3) for b in range(2)}
+        planes = {(w, b): held([P, 2 * PASSES * P], U8, f"planes{w}{b}") for w in (2, 3) for b in range(2)}
         left = [held([P, S], F32, f"left{i}") for i in range(PACK)]
         h = [held([P, S], F32, f"h{i}") for i in range(PACK)]
         g = [held([P, S], F32, f"g{i}") for i in range(PACK)]
@@ -68,61 +69,58 @@ def tile_list_berry_pair_order_kernel(
         gbias = held([P, PACK], F32, "gbias")
         a_look = [held([P, PAIRS], F32, f"a_look{i}") for i in range(PACK)]
         c_look = [held([P, PAIRS], F32, f"c_look{i}") for i in range(PACK)]
-        c_lead = [held([P, PAIRS], F32, f"c_lead{i}") for i in range(2)]
-        prod = [held([P, PAIRS], F32, f"prod{i}") for i in range(PACK)]
-        x32 = held([P, PACK, PAIRS], F32, "x32")
+        prod = held([P, PACK, PAIRS], F32, "prod")
         x_bf = [held([P, MH * PACK], BF16, f"x_bf{u}") for u in range(2)]
         x_w = [held([P, MH], U32, f"x_w{u}") for u in range(2)]
         x_s = [held([P, MH], U8, f"x_s{u}") for u in range(2)]
 
-        for a in range(PASSES):
-            nc.vector.memset(tab_s[a][:].bitcast(I32), 0)
+        nc.vector.memset(tab_s[:].bitcast(I32), 0)
         nc.gpsimd.memset(w1_sraw[:].bitcast(I32), 0)
+        nc.gpsimd.memset(v_s1[:].bitcast(I32), 0)
         nc.gpsimd.memset(w4_s[:].bitcast(I32), 0)
 
         def load_weight(w, src, a):
             rows = src[512 * a : 512 * (a + 1), :]
             nc.sync.dma_start(out=raw[w, a][:], in_=rows.rearrange("(p j) c -> p j c", j=PACK))
 
-        def load_tab_scales(a):
-            for q in range(QUADS):
-                nc.sync.dma_start(
-                    out=tab_s[a][32 * q : 32 * q + 4, :].bitcast(I32),
-                    in_=tab_scales[a, 4 * q : 4 * q + 4, :].bitcast(I32),
-                )
-
         nc.sync.dma_start(offs_sb[:], offs)
+        nc.sync.dma_start(
+            out=w1_raw[:].bitcast(I32).rearrange("p (a n) -> p a n", a=PASSES),
+            in_=w1_words.bitcast(I32).rearrange("a p n -> p a n"),
+        )
+        for q in range(QUADS):
+            nc.sync.dma_start(
+                out=tab_s[32 * q : 32 * q + 4 * PASSES, :].bitcast(I32),
+                in_=tab_scales[:, 4 * q : 4 * q + 4, :].bitcast(I32),
+            )
         nc.sync.dma_start(out=tab_w[0][:].bitcast(I32), in_=tab_words[0].rearrange("p n t -> p (n t)").bitcast(I32))
-        load_tab_scales(0)
-        nc.sync.dma_start(out=tab_w[1][:].bitcast(I32), in_=tab_words[1].rearrange("p n t -> p (n t)").bitcast(I32))
-        load_weight(3, w3, 0)
         for q in range(QUADS):
             nc.sync.dma_start(
                 out=w1_sraw[32 * q : 32 * q + 4, :].bitcast(I32).rearrange("r (a n) -> r a n", a=PASSES),
                 in_=w1_scales[:, 4 * q : 4 * q + 4, :].bitcast(I32).rearrange("a r n -> r a n"),
             )
-        load_weight(3, w3, 1)
-        load_tab_scales(1)
-        nc.sync.dma_start(
-            out=w1_raw[:].bitcast(I32).rearrange("p (a n) -> p a n", a=PASSES),
-            in_=w1_words.bitcast(I32).rearrange("a p n -> p a n"),
-        )
+        nc.sync.dma_start(out=tab_w[1][:].bitcast(I32), in_=tab_words[1].rearrange("p n t -> p (n t)").bitcast(I32))
+
+        nc.vector.tensor_copy(v_s[:], tab_s[:].indirect(offs_sb[:]))
+        nc.vector.tensor_copy(v_w[0][:], tab_w[0][:].indirect(offs_sb[:]))
+        nc.vector.tensor_copy(v_w[1][:], tab_w[1][:].indirect(offs_sb[:]))
+        for r in range(4):
+            nc.sync.dma_start(out=v_s1[r:P:32, :].bitcast(I32), in_=v_s[4 + r : P : 32, :].bitcast(I32))
+
         load_weight(2, w2, 0)
         load_weight(2, w2, 1)
-        nc.sync.dma_start(out=temp_sb[:], in_=temp.rearrange("(p i) -> p i", i=PACK))
-        nc.sync.dma_start(pos2_sb[:], pos2)
+        load_weight(3, w3, 0)
+        load_weight(3, w3, 1)
         nc.sync.dma_start(pos1_sb[:], pos1)
-        nc.sync.dma_start(out=lead_sb[:], in_=lead.rearrange("(p i) -> p i", i=PACK))
+        nc.sync.dma_start(out=temp_sb[:], in_=temp.rearrange("(p i) -> p i", i=PACK))
         nc.sync.dma_start(out=tray_sb[:], in_=tray.rearrange("(p i) m -> p i m", i=PACK))
+        nc.sync.dma_start(pos2_sb[:], pos2)
         nc.sync.dma_start(out=w4_w[:].bitcast(I32), in_=w4_words[0].rearrange("p n t -> p (n t)").bitcast(I32))
         for q in range(QUADS):
             nc.sync.dma_start(
                 out=w4_s[32 * q : 32 * q + 4, :].bitcast(I32), in_=w4_scales[0, 4 * q : 4 * q + 4, :].bitcast(I32)
             )
-
-        nc.vector.tensor_copy(v_w[0][:], tab_w[0][:].indirect(offs_sb[:]))
-        nc.vector.tensor_copy(v_s[0][:], tab_s[0][:].indirect(offs_sb[:]))
-        nc.vector.tensor_copy(v_w[1][:], tab_w[1][:].indirect(offs_sb[:]))
+        nc.sync.dma_start(out=lead_sb[:], in_=lead.rearrange("(p i) -> p i", i=PACK))
 
         nc.gpsimd.tensor_copy(
             w1_s[:].rearrange("p (a t c e) -> p a c t e", a=PASSES, t=PACK, e=4),
@@ -137,45 +135,49 @@ def tile_list_berry_pair_order_kernel(
                     lo = H * a + P * i
                     lhs = w1_w[:, lo : lo + P].bitcast(FP4X4)
                     lhs_s = w1_s[:, lo : lo + P]
+                    rhs_s = (v_s, v_s1)[a][:, cols]
                 else:
-                    lhs = codes[w, a][:, P * i : P * (i + 1)].bitcast(FP8X4)
-                    lhs_s = planes[w, a][:, P * i : P * (i + 1)]
+                    lo = P * (PASSES * (i % 2) + a)
+                    lhs = codes[w, i // 2][:, lo : lo + P].bitcast(FP8X4)
+                    lhs_s = planes[w, i // 2][:, lo : lo + P]
+                    rhs_s = v_s[4 * a : P, cols]
                 nc.tensor.matmul_mx(
-                    out=acc[:], lhsT=lhs, lhsT_scale=lhs_s, rhs=v_w[a][:, cols].bitcast(FP8X4), rhs_scale=v_s[a][:, cols],
+                    out=acc[:], lhsT=lhs, lhsT_scale=lhs_s, rhs=v_w[a][:, cols].bitcast(FP8X4), rhs_scale=rhs_s,
                     start=(a == 0), stop=(a == PASSES - 1),
                 )
             return acc
 
         def round_weight(copy, w, a, m0, m1):
             copy(
-                rounded[w, a][:, :, m0:m1, :].rearrange("p t m j -> p m t j"),
-                raw[w, a][:].rearrange("p j (m t) -> p m t j", t=PACK)[:, m0:m1, :, :],
+                rounded[w][:, :, a, m0:m1, :].rearrange("p t m j -> p m j t"),
+                raw[w, a][:].rearrange("p j (m t) -> p m j t", t=PACK)[:, m0:m1, :, :],
             )
 
-        def quantize_weight(w, a):
+        def quantize_weight(w, b):
             nc.vector.quantize_mx(
-                out=codes[w, a][:].bitcast(FP8X4), scales=planes[w, a][:],
-                in_=rounded[w, a][:].rearrange("p t m j -> p (t m j)"),
+                out=codes[w, b][:].bitcast(FP8X4), scales=planes[w, b][:],
+                in_=rounded[w][:, 2 * b : 2 * b + 2].rearrange("p t a m j -> p (t a m j)"),
             )
 
         def g_half(i, u):
             acc = product(3, i, u)
             col = HALVES * i + u
-            seed = None if u == 0 else gmax[:, col - 1 : col]
             nc.vector.tensor_scalar(
-                g[i][:, BANK * u : BANK * (u + 1)], acc[:], 1.0, seed, ALU.mult, ALU.max,
+                g[i][:, BANK * u : BANK * (u + 1)], acc[:], 1.0, None, ALU.mult, ALU.max,
                 accum_out=gmax[:, col : col + 1],
             )
 
-        def g_look(i):
-            col = HALVES * i + 1
-            nc.scalar.mul(gbias[:, i : i + 1], gmax[:, col : col + 1], ntemp[:, i : i + 1])
-            nc.scalar.activation(
-                c_look[i][:], g[i][:].indirect(pos2_sb[:]), ACT.Exp,
-                bias=gbias[:, i : i + 1], scale=temp_sb[:, i : i + 1],
+        def g_look(i, pieces):
+            col = HALVES * i
+            nc.vector.tensor_scalar(
+                gbias[:, i : i + 1], gmax[:, col : col + 1], gmax[:, col + 1 : col + 2], ntemp[:, i : i + 1],
+                ALU.max, ALU.mult,
             )
-            if i < 2:
-                nc.gpsimd.tensor_scalar(c_lead[i][:], c_look[i][:], lead_sb[:, i : i + 1], 0.0, ALU.mult, ALU.add)
+            for m0, m1 in pieces:
+                nc.scalar.activation(
+                    c_look[i][:, m0:m1], g[i][:].indirect(pos2_sb[:, m0 // 16 : m1 // 16]), ACT.Exp,
+                    bias=gbias[:, i : i + 1], scale=temp_sb[:, i : i + 1],
+                )
 
         def left_tile(i):
             for u in range(HALVES):
@@ -195,66 +197,68 @@ def tile_list_berry_pair_order_kernel(
                     bias=ntop[:, i : i + 1],
                 )
 
+        def join(i, m0, m1):
+            nc.vector.scalar_tensor_tensor(
+                prod[:, i, m0:m1], a_look[i][:, m0:m1], lead_sb[:, i : i + 1], c_look[i][:, m0:m1], ALU.mult, ALU.mult
+            )
+
         whole = [(0, PAIRS)]
         halves = [(0, MH), (MH, PAIRS)]
 
-        def gpsimd_round(dst, src):
-            nc.gpsimd.tensor_scalar(dst, src, 1.0, 0.0, ALU.mult, ALU.add)
-
-        round_weight(nc.scalar.copy, 3, 0, 0, P)
-        quantize_weight(3, 0)
-        round_weight(nc.scalar.copy, 3, 1, 0, P)
-        nc.vector.tensor_copy(v_s[1][:], tab_s[1][:].indirect(offs_sb[:]))
-        quantize_weight(3, 1)
         nc.scalar.copy(
             w1_w[:].rearrange("p (a t c e) -> p a c t e", a=PASSES, t=PACK, e=4),
             w1_raw[:].rearrange("p (a c e t) -> p a c t e", a=PASSES, t=PACK, e=4),
         )
-        for pair in range(2):
-            for u in range(HALVES):
-                g_half(2 * pair, u)
-                g_half(2 * pair + 1, u)
+        round_weight(nc.vector.tensor_copy, 2, 0, 0, P)
+        round_weight(nc.vector.tensor_copy, 2, 1, 0, P)
+        quantize_weight(2, 0)
         for i in range(PACK):
             left_tile(i)
-        for a in range(PASSES):
-            round_weight(gpsimd_round, 2, a, 0, P)
-            quantize_weight(2, a)
-        nc.scalar.mul(ntemp[:], temp_sb[:], -1.0)
+        quantize_weight(2, 1)
+        round_weight(nc.scalar.copy, 3, 0, 0, P)
+        round_weight(nc.scalar.copy, 3, 1, 0, P)
         h_half(0, 0)
         h_half(0, 1)
-        g_look(0)
         h_half(1, 0)
         h_look(0, whole)
         h_half(1, 1)
-        g_look(1)
-        nc.gpsimd.tensor_tensor(prod[0][:], a_look[0][:], c_lead[0][:], ALU.mult)
-        nc.gpsimd.tensor_tensor(x32[:, 0, :], prod[0][:], tray_sb[:, 0, :], ALU.add)
         h_half(2, 0)
         h_look(1, whole)
         h_half(2, 1)
-        g_look(2)
-        nc.gpsimd.tensor_tensor(prod[1][:], a_look[1][:], c_lead[1][:], ALU.mult)
-        nc.gpsimd.tensor_tensor(x32[:, 1, :], prod[1][:], tray_sb[:, 1, :], ALU.add)
-        h_half(3, 0)
+        quantize_weight(3, 0)
         h_look(2, whole)
+        h_half(3, 0)
         h_half(3, 1)
-        g_look(3)
-        h_look(3, halves)
-        nc.vector.scalar_tensor_tensor(prod[2][:], a_look[2][:], lead_sb[:, 2:3], c_look[2][:], ALU.mult, ALU.mult)
-        nc.vector.tensor_tensor(x32[:, 2, :], prod[2][:], tray_sb[:, 2, :], ALU.add)
+        quantize_weight(3, 1)
+        nc.vector.tensor_scalar(ntemp[:], temp_sb[:], -1.0, None, ALU.mult)
+        h_look(3, whole)
+        g_half(0, 0)
+        g_half(0, 1)
+        g_half(1, 0)
+        g_look(0, whole)
+        g_half(1, 1)
+        g_half(2, 0)
+        g_look(1, whole)
+        g_half(2, 1)
+        g_half(3, 0)
+        g_look(2, whole)
+        g_half(3, 1)
+        join(0, 0, PAIRS)
+        g_look(3, halves)
+        join(1, 0, PAIRS)
+        join(2, 0, PAIRS)
 
-        last = PACK - 1
         out_view = out.rearrange("(b p) m -> p b m", p=P)
+        join(3, 0, MH)
         for u, (m0, m1) in enumerate(halves):
-            nc.vector.scalar_tensor_tensor(
-                prod[last][:, m0:m1], a_look[last][:, m0:m1], lead_sb[:, last : last + 1], c_look[last][:, m0:m1],
-                ALU.mult, ALU.mult,
-            )
-            nc.vector.tensor_tensor(x32[:, last, m0:m1], prod[last][:, m0:m1], tray_sb[:, last, m0:m1], ALU.add)
-            (nc.vector.tensor_copy, nc.scalar.copy)[u](
+            nc.vector.tensor_tensor(
                 x_bf[u][:].rearrange("p (c e i) -> p c i e", e=4, i=PACK),
-                x32[:, :, m0:m1].rearrange("p i (c e) -> p c i e", e=4),
+                prod[:, :, m0:m1].rearrange("p i (c e) -> p c i e", e=4),
+                tray_sb[:, :, m0:m1].rearrange("p i (c e) -> p c i e", e=4),
+                ALU.add,
             )
+            if u == 0:
+                join(3, MH, PAIRS)
             nc.vector.quantize_mx(out=x_w[u][:].bitcast(FP8X4), scales=x_s[u][:], in_=x_bf[u][:])
             for b in range(2):
                 acc = psum.tile([P, BANK], F32, name="acc")
@@ -265,7 +269,7 @@ def tile_list_berry_pair_order_kernel(
                         rhs=x_w[u][:].bitcast(FP8X4), rhs_scale=x_s[u][:], start=True, stop=True,
                     )
                 res = held([P, BANK], F32, f"res{u}{b}")
-                if (u + b) % 2 == 0:
+                if u == 1 and b == 0:
                     nc.vector.tensor_copy(res[:], acc[:])
                 else:
                     nc.scalar.copy(res[:], acc[:])

@@ -57,10 +57,10 @@ def tile_list_berry_pair_order_kernel(
         ntemp = held([P, PACK], F32, "ntemp")
         lead_sb = held([P, PACK], F32, "lead_sb")
         tray_sb = held([P, PACK, PAIRS], F32, "tray_sb")
-        raw = {(w, a): held([P, PACK, H], F32, f"raw{w}{a}") for w in (2, 3) for a in range(PASSES)}
+        raw = {}
         rounded = {w: held([P, PACK, PASSES, P, PACK], BF16, f"rounded{w}") for w in (2, 3)}
-        codes = {(w, b): held([P, 2 * PASSES * P], U32, f"codes{w}{b}") for w in (2, 3) for b in range(2)}
-        planes = {(w, b): held([P, 2 * PASSES * P], U8, f"planes{w}{b}") for w in (2, 3) for b in range(2)}
+        codes = {w: held([P, PACK * PASSES * P], U32, f"codes{w}") for w in (2, 3)}
+        planes = {w: held([P, PACK * PASSES * P], U8, f"planes{w}") for w in (2, 3)}
         left = [held([P, S], F32, f"left{i}") for i in range(PACK)]
         h = [held([P, S], F32, f"h{i}") for i in range(PACK)]
         g = [held([P, S], F32, f"g{i}") for i in range(PACK)]
@@ -70,18 +70,17 @@ def tile_list_berry_pair_order_kernel(
         a_look = [held([P, PAIRS], F32, f"a_look{i}") for i in range(PACK)]
         c_look = [held([P, PAIRS], F32, f"c_look{i}") for i in range(PACK)]
         prod = held([P, PACK, PAIRS], F32, "prod")
-        x_bf = [held([P, MH * PACK], BF16, f"x_bf{u}") for u in range(2)]
-        x_w = [held([P, MH], U32, f"x_w{u}") for u in range(2)]
-        x_s = [held([P, MH], U8, f"x_s{u}") for u in range(2)]
 
         nc.vector.memset(tab_s[:].bitcast(I32), 0)
         nc.gpsimd.memset(w1_sraw[:].bitcast(I32), 0)
         nc.gpsimd.memset(v_s1[:].bitcast(I32), 0)
         nc.gpsimd.memset(w4_s[:].bitcast(I32), 0)
 
-        def load_weight(w, src, a):
-            rows = src[512 * a : 512 * (a + 1), :]
-            nc.sync.dma_start(out=raw[w, a][:], in_=rows.rearrange("(p j) c -> p j c", j=PACK))
+        def load_weight(w, src, a, m0, m1):
+            rows = src[512 * a : 512 * (a + 1), PACK * m0 : PACK * m1]
+            piece = held([P, PACK, PACK * (m1 - m0)], F32, f"raw{w}{a}{m0}")
+            raw[w, a, m0] = piece
+            nc.sync.dma_start(out=piece[:], in_=rows.rearrange("(p j) c -> p j c", j=PACK))
 
         nc.sync.dma_start(offs_sb[:], offs)
         nc.sync.dma_start(
@@ -102,15 +101,18 @@ def tile_list_berry_pair_order_kernel(
         nc.sync.dma_start(out=tab_w[1][:].bitcast(I32), in_=tab_words[1].rearrange("p n t -> p (n t)").bitcast(I32))
 
         nc.vector.tensor_copy(v_s[:], tab_s[:].indirect(offs_sb[:]))
-        nc.vector.tensor_copy(v_w[0][:], tab_w[0][:].indirect(offs_sb[:]))
-        nc.vector.tensor_copy(v_w[1][:], tab_w[1][:].indirect(offs_sb[:]))
+        for a in range(PASSES):
+            for u in range(HALVES):
+                entries = offs_sb[:, BANK // 16 * u : BANK // 16 * (u + 1)]
+                nc.vector.tensor_copy(v_w[a][:, BANK * u : BANK * (u + 1)], tab_w[a][:].indirect(entries))
+        load_weight(2, w2, 0, 0, P)
         for r in range(4):
             nc.sync.dma_start(out=v_s1[r:P:32, :].bitcast(I32), in_=v_s[4 + r : P : 32, :].bitcast(I32))
 
-        load_weight(2, w2, 0)
-        load_weight(2, w2, 1)
-        load_weight(3, w3, 0)
-        load_weight(3, w3, 1)
+        load_weight(2, w2, 1, 0, P // 2)
+        load_weight(2, w2, 1, P // 2, P)
+        load_weight(3, w3, 0, 0, P)
+        load_weight(3, w3, 1, 0, P)
         nc.sync.dma_start(pos1_sb[:], pos1)
         nc.sync.dma_start(out=temp_sb[:], in_=temp.rearrange("(p i) -> p i", i=PACK))
         nc.sync.dma_start(out=tray_sb[:], in_=tray.rearrange("(p i) m -> p i m", i=PACK))
@@ -122,10 +124,11 @@ def tile_list_berry_pair_order_kernel(
             )
         nc.sync.dma_start(out=lead_sb[:], in_=lead.rearrange("(p i) -> p i", i=PACK))
 
-        nc.gpsimd.tensor_copy(
-            w1_s[:].rearrange("p (a t c e) -> p a c t e", a=PASSES, t=PACK, e=4),
-            w1_sraw[:].rearrange("p (a c e t) -> p a c t e", a=PASSES, t=PACK, e=4),
-        )
+        for a in range(PASSES):
+            nc.gpsimd.tensor_copy(
+                w1_s[:, H * a : H * (a + 1)].rearrange("p (t c e) -> p c t e", t=PACK, e=4),
+                w1_sraw[:, H * a : H * (a + 1)].rearrange("p (c e t) -> p c t e", t=PACK, e=4),
+            )
 
         def product(w, i, u):
             acc = psum.tile([P, BANK], F32, name="acc")
@@ -137,9 +140,9 @@ def tile_list_berry_pair_order_kernel(
                     lhs_s = w1_s[:, lo : lo + P]
                     rhs_s = (v_s, v_s1)[a][:, cols]
                 else:
-                    lo = P * (PASSES * (i % 2) + a)
-                    lhs = codes[w, i // 2][:, lo : lo + P].bitcast(FP8X4)
-                    lhs_s = planes[w, i // 2][:, lo : lo + P]
+                    lo = P * (PASSES * i + a)
+                    lhs = codes[w][:, lo : lo + P].bitcast(FP8X4)
+                    lhs_s = planes[w][:, lo : lo + P]
                     rhs_s = v_s[4 * a : P, cols]
                 nc.tensor.matmul_mx(
                     out=acc[:], lhsT=lhs, lhsT_scale=lhs_s, rhs=v_w[a][:, cols].bitcast(FP8X4), rhs_scale=rhs_s,
@@ -147,16 +150,17 @@ def tile_list_berry_pair_order_kernel(
                 )
             return acc
 
-        def round_weight(copy, w, a, m0, m1):
+        def round_weight(copy, w, a, first, m0, m1):
             copy(
                 rounded[w][:, :, a, m0:m1, :].rearrange("p t m j -> p m j t"),
-                raw[w, a][:].rearrange("p j (m t) -> p m j t", t=PACK)[:, m0:m1, :, :],
+                raw[w, a, first][:].rearrange("p j (m t) -> p m j t", t=PACK)[:, m0 - first : m1 - first],
             )
 
-        def quantize_weight(w, b):
+        def quantize_weight(w, i0, i1):
+            cols = slice(PASSES * P * i0, PASSES * P * i1)
             nc.vector.quantize_mx(
-                out=codes[w, b][:].bitcast(FP8X4), scales=planes[w, b][:],
-                in_=rounded[w][:, 2 * b : 2 * b + 2].rearrange("p t a m j -> p (t a m j)"),
+                out=codes[w][:, cols].bitcast(FP8X4), scales=planes[w][:, cols],
+                in_=rounded[w][:, i0:i1].rearrange("p t a m j -> p (t a m j)"),
             )
 
         def g_half(i, u):
@@ -179,10 +183,9 @@ def tile_list_berry_pair_order_kernel(
                     bias=gbias[:, i : i + 1], scale=temp_sb[:, i : i + 1],
                 )
 
-        def left_tile(i):
-            for u in range(HALVES):
-                acc = product(1, i, u)
-                nc.scalar.copy(left[i][:, BANK * u : BANK * (u + 1)], acc[:])
+        def left_half(i, u):
+            acc = product(1, i, u)
+            nc.scalar.copy(left[i][:, BANK * u : BANK * (u + 1)], acc[:])
 
         def h_half(i, u):
             acc = product(2, i, u)
@@ -209,14 +212,18 @@ def tile_list_berry_pair_order_kernel(
             w1_w[:].rearrange("p (a t c e) -> p a c t e", a=PASSES, t=PACK, e=4),
             w1_raw[:].rearrange("p (a c e t) -> p a c t e", a=PASSES, t=PACK, e=4),
         )
-        round_weight(nc.vector.tensor_copy, 2, 0, 0, P)
-        round_weight(nc.vector.tensor_copy, 2, 1, 0, P)
-        quantize_weight(2, 0)
-        for i in range(PACK):
-            left_tile(i)
-        quantize_weight(2, 1)
-        round_weight(nc.scalar.copy, 3, 0, 0, P)
-        round_weight(nc.scalar.copy, 3, 1, 0, P)
+        round_weight(nc.scalar.copy, 2, 0, 0, 0, 96)
+        round_weight(nc.vector.tensor_copy, 2, 0, 0, 96, P)
+        round_weight(nc.vector.tensor_copy, 2, 1, 0, 0, P // 2)
+        round_weight(nc.vector.tensor_copy, 2, 1, P // 2, P // 2, P)
+        quantize_weight(2, 0, 1)
+        quantize_weight(2, 1, 2)
+        for u in range(HALVES):
+            for i in range(PACK):
+                left_half(i, u)
+        quantize_weight(2, 2, 4)
+        round_weight(nc.scalar.copy, 3, 0, 0, 0, P)
+        round_weight(nc.scalar.copy, 3, 1, 0, 0, P)
         h_half(0, 0)
         h_half(0, 1)
         h_half(1, 0)
@@ -225,11 +232,11 @@ def tile_list_berry_pair_order_kernel(
         h_half(2, 0)
         h_look(1, whole)
         h_half(2, 1)
-        quantize_weight(3, 0)
+        quantize_weight(3, 0, 2)
         h_look(2, whole)
         h_half(3, 0)
         h_half(3, 1)
-        quantize_weight(3, 1)
+        quantize_weight(3, 2, 4)
         nc.vector.tensor_scalar(ntemp[:], temp_sb[:], -1.0, None, ALU.mult)
         h_look(3, whole)
         g_half(0, 0)
@@ -249,30 +256,44 @@ def tile_list_berry_pair_order_kernel(
         join(2, 0, PAIRS)
 
         out_view = out.rearrange("(b p) m -> p b m", p=P)
-        join(3, 0, MH)
-        for u, (m0, m1) in enumerate(halves):
+
+        def round_x(m0, m1):
+            x_bf = held([P, (m1 - m0) * PACK], BF16, f"x_bf{m0}")
             nc.vector.tensor_tensor(
-                x_bf[u][:].rearrange("p (c e i) -> p c i e", e=4, i=PACK),
+                x_bf[:].rearrange("p (c e i) -> p c i e", e=4, i=PACK),
                 prod[:, :, m0:m1].rearrange("p i (c e) -> p c i e", e=4),
                 tray_sb[:, :, m0:m1].rearrange("p i (c e) -> p c i e", e=4),
                 ALU.add,
             )
-            if u == 0:
-                join(3, MH, PAIRS)
-            nc.vector.quantize_mx(out=x_w[u][:].bitcast(FP8X4), scales=x_s[u][:], in_=x_bf[u][:])
-            for b in range(2):
+            return x_bf
+
+        def last_product(x_bf, m0, m1, copies):
+            width = m1 - m0
+            x_w = held([P, width], U32, f"x_w{m0}")
+            x_s = held([P, width], U8, f"x_s{m0}")
+            nc.vector.quantize_mx(out=x_w[:].bitcast(FP8X4), scales=x_s[:], in_=x_bf[:])
+            per_bank = PACK // len(copies)
+            for b, copy in enumerate(copies):
                 acc = psum.tile([P, BANK], F32, name="acc")
-                for s in range(2):
-                    cols = slice(P * (2 * b + s), P * (2 * b + s + 1))
+                for s in range(per_bank):
+                    cols = slice(P * (per_bank * b + s), P * (per_bank * b + s + 1))
                     nc.tensor.matmul_mx(
-                        out=acc[:, MH * s : MH * (s + 1)], lhsT=w4_w[:, cols].bitcast(FP8X4), lhsT_scale=w4_s[:, cols],
-                        rhs=x_w[u][:].bitcast(FP8X4), rhs_scale=x_s[u][:], start=True, stop=True,
+                        out=acc[:, width * s : width * (s + 1)], lhsT=w4_w[:, cols].bitcast(FP8X4),
+                        lhsT_scale=w4_s[:, cols], rhs=x_w[:].bitcast(FP8X4), rhs_scale=x_s[:], start=True, stop=True,
                     )
-                res = held([P, BANK], F32, f"res{u}{b}")
-                if u == 1 and b == 0:
-                    nc.vector.tensor_copy(res[:], acc[:])
-                else:
-                    nc.scalar.copy(res[:], acc[:])
+                res = held([P, per_bank * width], F32, f"res{m0}{b}")
+                copy(res[:], acc[:, 0 : per_bank * width])
                 nc.sync.dma_start(
-                    out=out_view[:, 2 * b : 2 * b + 2, m0:m1], in_=res[:].rearrange("p (s m) -> p s m", s=2)
+                    out=out_view[:, per_bank * b : per_bank * (b + 1), m0:m1],
+                    in_=res[:].rearrange("p (s m) -> p s m", s=per_bank),
                 )
+
+        third = MH + MH // 2
+        join(3, 0, MH)
+        x0 = round_x(0, MH)
+        join(3, MH, PAIRS)
+        last_product(x0, 0, MH, (nc.scalar.copy, nc.scalar.copy))
+        x1 = round_x(MH, third)
+        x2 = round_x(third, PAIRS)
+        last_product(x1, MH, third, (nc.vector.tensor_copy,))
+        last_product(x2, third, PAIRS, (nc.scalar.copy, nc.vector.tensor_copy))

@@ -19,11 +19,19 @@ AXIS = mybir.AxisListType
 
 P = 128
 PACK = 4
-PASSES = K // (P * PACK)
+K_PASS = P * PACK
+PASSES = K // K_PASS
 QUADS = 4
+QUAD = P // QUADS
+LIVE = 4
+LIST_ROWS = 16
+RUN = 4
 BANK = 512
 HALVES = S // BANK
 MH = PAIRS // 2
+LAST = PACK - 1
+SCALAR_SHARE = 96
+PACED_BANKS = 3
 
 
 def tile_list_berry_pair_order_kernel(
@@ -33,14 +41,15 @@ def tile_list_berry_pair_order_kernel(
     with ExitStack() as ctx:
         lists = ctx.enter_context(tc.tile_pool(name="lists", bufs=1))
         keep = ctx.enter_context(tc.tile_pool(name="keep", bufs=1))
-        psum = ctx.enter_context(tc.psum_pool(name="psum", bufs=8))
+        psum = ctx.enter_context(tc.psum_pool(name="psum", bufs=8 - PACED_BANKS))
+        paced = ctx.enter_context(tc.psum_pool(name="paced", bufs=PACED_BANKS))
 
         def held(shape, dtype, name):
             return keep.tile(shape, dtype, name=name, align_bytes=64)
 
-        offs_sb = lists.tile([P, S // 16], U16, name="offs_sb")
-        pos1_sb = lists.tile([P, PAIRS // 16], U16, name="pos1_sb")
-        pos2_sb = lists.tile([P, PAIRS // 16], U16, name="pos2_sb")
+        offs_sb = lists.tile([P, S // LIST_ROWS], U16, name="offs_sb")
+        pos1_sb = lists.tile([P, PAIRS // LIST_ROWS], U16, name="pos1_sb")
+        pos2_sb = lists.tile([P, PAIRS // LIST_ROWS], U16, name="pos2_sb")
 
         tab_w = [held([P, T], U32, f"tab_w{a}") for a in range(PASSES)]
         tab_s = held([P, T], U8, "tab_s")
@@ -77,7 +86,7 @@ def tile_list_berry_pair_order_kernel(
         nc.gpsimd.memset(w4_s[:].bitcast(I32), 0)
 
         def load_weight(w, src, a, m0, m1):
-            rows = src[512 * a : 512 * (a + 1), PACK * m0 : PACK * m1]
+            rows = src[K_PASS * a : K_PASS * (a + 1), PACK * m0 : PACK * m1]
             piece = held([P, PACK, PACK * (m1 - m0)], F32, f"raw{w}{a}{m0}")
             raw[w, a, m0] = piece
             nc.sync.dma_start(out=piece[:], in_=rows.rearrange("(p j) c -> p j c", j=PACK))
@@ -89,25 +98,25 @@ def tile_list_berry_pair_order_kernel(
         )
         for q in range(QUADS):
             nc.sync.dma_start(
-                out=tab_s[32 * q : 32 * q + 4 * PASSES, :].bitcast(I32),
-                in_=tab_scales[:, 4 * q : 4 * q + 4, :].bitcast(I32),
+                out=tab_s[QUAD * q : QUAD * q + LIVE * PASSES, :].bitcast(I32),
+                in_=tab_scales[:, LIVE * q : LIVE * (q + 1), :].bitcast(I32),
             )
         nc.sync.dma_start(out=tab_w[0][:].bitcast(I32), in_=tab_words[0].rearrange("p n t -> p (n t)").bitcast(I32))
         for q in range(QUADS):
             nc.sync.dma_start(
-                out=w1_sraw[32 * q : 32 * q + 4, :].bitcast(I32).rearrange("r (a n) -> r a n", a=PASSES),
-                in_=w1_scales[:, 4 * q : 4 * q + 4, :].bitcast(I32).rearrange("a r n -> r a n"),
+                out=w1_sraw[QUAD * q : QUAD * q + LIVE, :].bitcast(I32).rearrange("r (a n) -> r a n", a=PASSES),
+                in_=w1_scales[:, LIVE * q : LIVE * (q + 1), :].bitcast(I32).rearrange("a r n -> r a n"),
             )
         nc.sync.dma_start(out=tab_w[1][:].bitcast(I32), in_=tab_words[1].rearrange("p n t -> p (n t)").bitcast(I32))
 
         nc.vector.tensor_copy(v_s[:], tab_s[:].indirect(offs_sb[:]))
         for a in range(PASSES):
             for u in range(HALVES):
-                entries = offs_sb[:, BANK // 16 * u : BANK // 16 * (u + 1)]
+                entries = offs_sb[:, BANK // LIST_ROWS * u : BANK // LIST_ROWS * (u + 1)]
                 nc.vector.tensor_copy(v_w[a][:, BANK * u : BANK * (u + 1)], tab_w[a][:].indirect(entries))
         load_weight(2, w2, 0, 0, P)
-        for r in range(4):
-            nc.sync.dma_start(out=v_s1[r:P:32, :].bitcast(I32), in_=v_s[4 + r : P : 32, :].bitcast(I32))
+        for s in range(LIVE):
+            nc.sync.dma_start(out=v_s1[s:P:QUAD, :].bitcast(I32), in_=v_s[LIVE + s : P : QUAD, :].bitcast(I32))
 
         load_weight(2, w2, 1, 0, P // 2)
         load_weight(2, w2, 1, P // 2, P)
@@ -120,18 +129,20 @@ def tile_list_berry_pair_order_kernel(
         nc.sync.dma_start(out=w4_w[:].bitcast(I32), in_=w4_words[0].rearrange("p n t -> p (n t)").bitcast(I32))
         for q in range(QUADS):
             nc.sync.dma_start(
-                out=w4_s[32 * q : 32 * q + 4, :].bitcast(I32), in_=w4_scales[0, 4 * q : 4 * q + 4, :].bitcast(I32)
+                out=w4_s[QUAD * q : QUAD * q + LIVE, :].bitcast(I32),
+                in_=w4_scales[0, LIVE * q : LIVE * (q + 1), :].bitcast(I32),
             )
         nc.sync.dma_start(out=lead_sb[:], in_=lead.rearrange("(p i) -> p i", i=PACK))
 
         for a in range(PASSES):
             nc.gpsimd.tensor_copy(
-                w1_s[:, H * a : H * (a + 1)].rearrange("p (t c e) -> p c t e", t=PACK, e=4),
-                w1_sraw[:, H * a : H * (a + 1)].rearrange("p (c e t) -> p c t e", t=PACK, e=4),
+                w1_s[:, H * a : H * (a + 1)].rearrange("p (t c e) -> p c t e", t=PACK, e=RUN),
+                w1_sraw[:, H * a : H * (a + 1)].rearrange("p (c e t) -> p c t e", t=PACK, e=RUN),
             )
 
         def product(w, i, u):
-            acc = psum.tile([P, BANK], F32, name="acc")
+            banks = paced if w == 2 or (w == 1 and u == 0 and i < PACED_BANKS) else psum
+            acc = banks.tile([P, BANK], F32, name="acc")
             cols = slice(BANK * u, BANK * (u + 1))
             for a in range(PASSES):
                 if w == 1:
@@ -143,7 +154,7 @@ def tile_list_berry_pair_order_kernel(
                     lo = P * (PASSES * i + a)
                     lhs = codes[w][:, lo : lo + P].bitcast(FP8X4)
                     lhs_s = planes[w][:, lo : lo + P]
-                    rhs_s = v_s[4 * a : P, cols]
+                    rhs_s = v_s[LIVE * a : P, cols]
                 nc.tensor.matmul_mx(
                     out=acc[:], lhsT=lhs, lhsT_scale=lhs_s, rhs=v_w[a][:, cols].bitcast(FP8X4), rhs_scale=rhs_s,
                     start=(a == 0), stop=(a == PASSES - 1),
@@ -179,7 +190,7 @@ def tile_list_berry_pair_order_kernel(
             )
             for m0, m1 in pieces:
                 nc.scalar.activation(
-                    c_look[i][:, m0:m1], g[i][:].indirect(pos2_sb[:, m0 // 16 : m1 // 16]), ACT.Exp,
+                    c_look[i][:, m0:m1], g[i][:].indirect(pos2_sb[:, m0 // LIST_ROWS : m1 // LIST_ROWS]), ACT.Exp,
                     bias=gbias[:, i : i + 1], scale=temp_sb[:, i : i + 1],
                 )
 
@@ -192,28 +203,21 @@ def tile_list_berry_pair_order_kernel(
             cols = slice(BANK * u, BANK * (u + 1))
             nc.vector.tensor_tensor(h[i][:, cols], left[i][:, cols], acc[:], ALU.max)
 
-        def h_look(i, pieces):
+        def h_look(i):
             nc.vector.tensor_reduce(ntop[:, i : i + 1], h[i][:], AXIS.X, ALU.max, negate=True)
-            for m0, m1 in pieces:
-                nc.scalar.activation(
-                    a_look[i][:, m0:m1], h[i][:].indirect(pos1_sb[:, m0 // 16 : m1 // 16]), ACT.Exp,
-                    bias=ntop[:, i : i + 1],
-                )
+            nc.scalar.activation(a_look[i][:], h[i][:].indirect(pos1_sb[:]), ACT.Exp, bias=ntop[:, i : i + 1])
 
         def join(i, m0, m1):
             nc.vector.scalar_tensor_tensor(
                 prod[:, i, m0:m1], a_look[i][:, m0:m1], lead_sb[:, i : i + 1], c_look[i][:, m0:m1], ALU.mult, ALU.mult
             )
 
-        whole = [(0, PAIRS)]
-        halves = [(0, MH), (MH, PAIRS)]
-
         nc.scalar.copy(
-            w1_w[:].rearrange("p (a t c e) -> p a c t e", a=PASSES, t=PACK, e=4),
-            w1_raw[:].rearrange("p (a c e t) -> p a c t e", a=PASSES, t=PACK, e=4),
+            w1_w[:].rearrange("p (a t c e) -> p a c t e", a=PASSES, t=PACK, e=RUN),
+            w1_raw[:].rearrange("p (a c e t) -> p a c t e", a=PASSES, t=PACK, e=RUN),
         )
-        round_weight(nc.scalar.copy, 2, 0, 0, 0, 96)
-        round_weight(nc.vector.tensor_copy, 2, 0, 0, 96, P)
+        round_weight(nc.scalar.copy, 2, 0, 0, 0, SCALAR_SHARE)
+        round_weight(nc.vector.tensor_copy, 2, 0, 0, SCALAR_SHARE, P)
         round_weight(nc.vector.tensor_copy, 2, 1, 0, 0, P // 2)
         round_weight(nc.vector.tensor_copy, 2, 1, P // 2, P // 2, P)
         quantize_weight(2, 0, 1)
@@ -221,48 +225,43 @@ def tile_list_berry_pair_order_kernel(
         for u in range(HALVES):
             for i in range(PACK):
                 left_half(i, u)
-        quantize_weight(2, 2, 4)
-        round_weight(nc.scalar.copy, 3, 0, 0, 0, P)
-        round_weight(nc.scalar.copy, 3, 1, 0, 0, P)
+        quantize_weight(2, 2, PACK)
+        for a in range(PASSES):
+            round_weight(nc.scalar.copy, 3, a, 0, 0, P)
+
         h_half(0, 0)
-        h_half(0, 1)
-        h_half(1, 0)
-        h_look(0, whole)
-        h_half(1, 1)
-        h_half(2, 0)
-        h_look(1, whole)
-        h_half(2, 1)
+        for i in range(LAST - 1):
+            h_half(i, 1)
+            h_half(i + 1, 0)
+            h_look(i)
+        h_half(LAST - 1, 1)
         quantize_weight(3, 0, 2)
-        h_look(2, whole)
-        h_half(3, 0)
-        h_half(3, 1)
-        quantize_weight(3, 2, 4)
+        h_look(LAST - 1)
+        h_half(LAST, 0)
+        h_half(LAST, 1)
+        quantize_weight(3, 2, PACK)
         nc.vector.tensor_scalar(ntemp[:], temp_sb[:], -1.0, None, ALU.mult)
-        h_look(3, whole)
+        h_look(LAST)
+
         g_half(0, 0)
-        g_half(0, 1)
-        g_half(1, 0)
-        g_look(0, whole)
-        g_half(1, 1)
-        g_half(2, 0)
-        g_look(1, whole)
-        g_half(2, 1)
-        g_half(3, 0)
-        g_look(2, whole)
-        g_half(3, 1)
+        for i in range(LAST):
+            g_half(i, 1)
+            g_half(i + 1, 0)
+            g_look(i, [(0, PAIRS)])
+        g_half(LAST, 1)
         join(0, 0, PAIRS)
-        g_look(3, halves)
-        join(1, 0, PAIRS)
-        join(2, 0, PAIRS)
+        g_look(LAST, [(0, MH), (MH, PAIRS)])
+        for i in range(1, LAST):
+            join(i, 0, PAIRS)
 
         out_view = out.rearrange("(b p) m -> p b m", p=P)
 
         def round_x(m0, m1):
             x_bf = held([P, (m1 - m0) * PACK], BF16, f"x_bf{m0}")
             nc.vector.tensor_tensor(
-                x_bf[:].rearrange("p (c e i) -> p c i e", e=4, i=PACK),
-                prod[:, :, m0:m1].rearrange("p i (c e) -> p c i e", e=4),
-                tray_sb[:, :, m0:m1].rearrange("p i (c e) -> p c i e", e=4),
+                x_bf[:].rearrange("p (c e i) -> p c i e", e=RUN, i=PACK),
+                prod[:, :, m0:m1].rearrange("p i (c e) -> p c i e", e=RUN),
+                tray_sb[:, :, m0:m1].rearrange("p i (c e) -> p c i e", e=RUN),
                 ALU.add,
             )
             return x_bf
@@ -272,28 +271,28 @@ def tile_list_berry_pair_order_kernel(
             x_w = held([P, width], U32, f"x_w{m0}")
             x_s = held([P, width], U8, f"x_s{m0}")
             nc.vector.quantize_mx(out=x_w[:].bitcast(FP8X4), scales=x_s[:], in_=x_bf[:])
-            per_bank = PACK // len(copies)
+            per_bank = N // P // len(copies)
             for b, copy in enumerate(copies):
                 acc = psum.tile([P, BANK], F32, name="acc")
-                for s in range(per_bank):
-                    cols = slice(P * (per_bank * b + s), P * (per_bank * b + s + 1))
+                for place in range(per_bank):
+                    cols = slice(P * (per_bank * b + place), P * (per_bank * b + place + 1))
                     nc.tensor.matmul_mx(
-                        out=acc[:, width * s : width * (s + 1)], lhsT=w4_w[:, cols].bitcast(FP8X4),
+                        out=acc[:, width * place : width * (place + 1)], lhsT=w4_w[:, cols].bitcast(FP8X4),
                         lhsT_scale=w4_s[:, cols], rhs=x_w[:].bitcast(FP8X4), rhs_scale=x_s[:], start=True, stop=True,
                     )
                 res = held([P, per_bank * width], F32, f"res{m0}{b}")
                 copy(res[:], acc[:, 0 : per_bank * width])
                 nc.sync.dma_start(
                     out=out_view[:, per_bank * b : per_bank * (b + 1), m0:m1],
-                    in_=res[:].rearrange("p (s m) -> p s m", s=per_bank),
+                    in_=res[:].rearrange("p (b m) -> p b m", b=per_bank),
                 )
 
-        third = MH + MH // 2
-        join(3, 0, MH)
+        quarter = MH + MH // 2
+        join(LAST, 0, MH)
         x0 = round_x(0, MH)
-        join(3, MH, PAIRS)
+        join(LAST, MH, PAIRS)
         last_product(x0, 0, MH, (nc.scalar.copy, nc.scalar.copy))
-        x1 = round_x(MH, third)
-        x2 = round_x(third, PAIRS)
-        last_product(x1, MH, third, (nc.vector.tensor_copy,))
-        last_product(x2, third, PAIRS, (nc.scalar.copy, nc.vector.tensor_copy))
+        x1 = round_x(MH, quarter)
+        x2 = round_x(quarter, PAIRS)
+        last_product(x1, MH, quarter, (nc.vector.tensor_copy,))
+        last_product(x2, quarter, PAIRS, (nc.scalar.copy, nc.vector.tensor_copy))

from contextlib import ExitStack

import concourse.mybir as mybir

K, T, S, H, PAIRS, N = 1024, 2048, 1024, 512, 512, 512
FLOPS = 3 * 2 * K * H * S + 2 * H * N * PAIRS

F32 = mybir.dt.float32
BF16 = mybir.dt.bfloat16
I32 = mybir.dt.int32
U32 = mybir.dt.uint32
U16 = mybir.dt.uint16
U8 = mybir.dt.uint8
FP8X4 = mybir.dt.float8_e4m3fn_x4
FP4X4 = mybir.dt.float4_e2m1fn_x4
ALU = mybir.AluOpType
ACT = mybir.ActivationFunctionType
AXIS = mybir.AxisListType

P = 128
PACK = 4
K_PASS = P * PACK
PASSES = K // K_PASS
QUADS = 4
QUAD = P // QUADS
LIVE = 4
LIST_ROWS = 16
RUN = 4
BANK = 512
HALVES = S // BANK
MH = PAIRS // 2
LAST = PACK - 1
SCALAR_SHARE = 96
PACED_BANKS = 3


def tile_list_berry_pair_order_kernel(
    tc, tab_words, tab_scales, offs, pos1, pos2, w1_words, w1_scales, w2, w3, temp, lead, tray, w4_words, w4_scales, out
):
    nc = tc.nc
    with ExitStack() as ctx:
        lists = ctx.enter_context(tc.tile_pool(name="lists", bufs=1))
        keep = ctx.enter_context(tc.tile_pool(name="keep", bufs=1))
        psum = ctx.enter_context(tc.psum_pool(name="psum", bufs=8 - PACED_BANKS))
        paced = ctx.enter_context(tc.psum_pool(name="paced", bufs=PACED_BANKS))

        def held(shape, dtype, name):
            return keep.tile(shape, dtype, name=name, align_bytes=64)

        offs_sb = lists.tile([P, S // LIST_ROWS], U16, name="offs_sb")
        pos1_sb = lists.tile([P, PAIRS // LIST_ROWS], U16, name="pos1_sb")
        pos2_sb = lists.tile([P, PAIRS // LIST_ROWS], U16, name="pos2_sb")

        tab_w = [held([P, T], U32, f"tab_w{a}") for a in range(PASSES)]
        tab_s = held([P, T], U8, "tab_s")
        v_w = [held([P, S], U32, f"v_w{a}") for a in range(PASSES)]
        v_s = held([P, S], U8, "v_s")
        v_s1 = held([P, S], U8, "v_s1")
        w1_raw = held([P, PASSES * H], U16, "w1_raw")
        w1_w = held([P, PASSES * H], U16, "w1_w")
        w1_sraw = held([P, PASSES * H], U8, "w1_sraw")
        w1_s = held([P, PASSES * H], U8, "w1_s")
        w4_w = held([P, N], U32, "w4_w")
        w4_s = held([P, N], U8, "w4_s")
        temp_sb = held([P, PACK], F32, "temp_sb")
        ntemp = held([P, PACK], F32, "ntemp")
        lead_sb = held([P, PACK], F32, "lead_sb")
        tray_sb = held([P, PACK, PAIRS], F32, "tray_sb")
        raw = {}
        rounded = {w: held([P, PACK, PASSES, P, PACK], BF16, f"rounded{w}") for w in (2, 3)}
        codes = {w: held([P, PACK * PASSES * P], U32, f"codes{w}") for w in (2, 3)}
        planes = {w: held([P, PACK * PASSES * P], U8, f"planes{w}") for w in (2, 3)}
        left = [held([P, S], F32, f"left{i}") for i in range(PACK)]
        h = [held([P, S], F32, f"h{i}") for i in range(PACK)]
        g = [held([P, S], F32, f"g{i}") for i in range(PACK)]
        ntop = held([P, PACK], F32, "ntop")
        gmax = held([P, PACK * HALVES], F32, "gmax")
        gbias = held([P, PACK], F32, "gbias")
        a_look = [held([P, PAIRS], F32, f"a_look{i}") for i in range(PACK)]
        c_look = [held([P, PAIRS], F32, f"c_look{i}") for i in range(PACK)]
        prod = held([P, PACK, PAIRS], F32, "prod")

        nc.vector.memset(tab_s[:].bitcast(I32), 0)
        nc.gpsimd.memset(w1_sraw[:].bitcast(I32), 0)
        nc.gpsimd.memset(v_s1[:].bitcast(I32), 0)
        nc.gpsimd.memset(w4_s[:].bitcast(I32), 0)

        def load_weight(w, src, a, m0, m1):
            rows = src[K_PASS * a : K_PASS * (a + 1), PACK * m0 : PACK * m1]
            piece = held([P, PACK, PACK * (m1 - m0)], F32, f"raw{w}{a}{m0}")
            raw[w, a, m0] = piece
            nc.sync.dma_start(out=piece[:], in_=rows.rearrange("(p j) c -> p j c", j=PACK))

        nc.sync.dma_start(offs_sb[:], offs)
        nc.sync.dma_start(
            out=w1_raw[:].bitcast(I32).rearrange("p (a n) -> p a n", a=PASSES),
            in_=w1_words.bitcast(I32).rearrange("a p n -> p a n"),
        )
        for q in range(QUADS):
            nc.sync.dma_start(
                out=tab_s[QUAD * q : QUAD * q + LIVE * PASSES, :].bitcast(I32),
                in_=tab_scales[:, LIVE * q : LIVE * (q + 1), :].bitcast(I32),
            )
        nc.sync.dma_start(out=tab_w[0][:].bitcast(I32), in_=tab_words[0].rearrange("p n t -> p (n t)").bitcast(I32))
        for q in range(QUADS):
            nc.sync.dma_start(
                out=w1_sraw[QUAD * q : QUAD * q + LIVE, :].bitcast(I32).rearrange("r (a n) -> r a n", a=PASSES),
                in_=w1_scales[:, LIVE * q : LIVE * (q + 1), :].bitcast(I32).rearrange("a r n -> r a n"),
            )
        nc.sync.dma_start(out=tab_w[1][:].bitcast(I32), in_=tab_words[1].rearrange("p n t -> p (n t)").bitcast(I32))

        nc.vector.tensor_copy(v_s[:], tab_s[:].indirect(offs_sb[:]))
        for a in range(PASSES):
            for u in range(HALVES):
                entries = offs_sb[:, BANK // LIST_ROWS * u : BANK // LIST_ROWS * (u + 1)]
                nc.vector.tensor_copy(v_w[a][:, BANK * u : BANK * (u + 1)], tab_w[a][:].indirect(entries))
        load_weight(2, w2, 0, 0, P)
        for s in range(LIVE):
            nc.sync.dma_start(out=v_s1[s:P:QUAD, :].bitcast(I32), in_=v_s[LIVE + s : P : QUAD, :].bitcast(I32))

        load_weight(2, w2, 1, 0, P // 2)
        load_weight(2, w2, 1, P // 2, P)
        load_weight(3, w3, 0, 0, P)
        load_weight(3, w3, 1, 0, P)
        nc.sync.dma_start(pos1_sb[:], pos1)
        nc.sync.dma_start(out=temp_sb[:], in_=temp.rearrange("(p i) -> p i", i=PACK))
        nc.sync.dma_start(out=tray_sb[:], in_=tray.rearrange("(p i) m -> p i m", i=PACK))
        nc.sync.dma_start(pos2_sb[:], pos2)
        nc.sync.dma_start(out=w4_w[:].bitcast(I32), in_=w4_words[0].rearrange("p n t -> p (n t)").bitcast(I32))
        for q in range(QUADS):
            nc.sync.dma_start(
                out=w4_s[QUAD * q : QUAD * q + LIVE, :].bitcast(I32),
                in_=w4_scales[0, LIVE * q : LIVE * (q + 1), :].bitcast(I32),
            )
        nc.sync.dma_start(out=lead_sb[:], in_=lead.rearrange("(p i) -> p i", i=PACK))

        for a in range(PASSES):
            nc.gpsimd.tensor_copy(
                w1_s[:, H * a : H * (a + 1)].rearrange("p (t c e) -> p c t e", t=PACK, e=RUN),
                w1_sraw[:, H * a : H * (a + 1)].rearrange("p (c e t) -> p c t e", t=PACK, e=RUN),
            )

        def product(w, i, u):
            banks = paced if w == 2 or (w == 1 and u == 0 and i < PACED_BANKS) else psum
            acc = banks.tile([P, BANK], F32, name="acc")
            cols = slice(BANK * u, BANK * (u + 1))
            for a in range(PASSES):
                if w == 1:
                    lo = H * a + P * i
                    lhs = w1_w[:, lo : lo + P].bitcast(FP4X4)
                    lhs_s = w1_s[:, lo : lo + P]
                    rhs_s = (v_s, v_s1)[a][:, cols]
                else:
                    lo = P * (PASSES * i + a)
                    lhs = codes[w][:, lo : lo + P].bitcast(FP8X4)
                    lhs_s = planes[w][:, lo : lo + P]
                    rhs_s = v_s[LIVE * a : P, cols]
                nc.tensor.matmul_mx(
                    out=acc[:], lhsT=lhs, lhsT_scale=lhs_s, rhs=v_w[a][:, cols].bitcast(FP8X4), rhs_scale=rhs_s,
                    start=(a == 0), stop=(a == PASSES - 1),
                )
            return acc

        def round_weight(copy, w, a, first, m0, m1):
            copy(
                rounded[w][:, :, a, m0:m1, :].rearrange("p t m j -> p m j t"),
                raw[w, a, first][:].rearrange("p j (m t) -> p m j t", t=PACK)[:, m0 - first : m1 - first],
            )

        def quantize_weight(w, i0, i1):
            cols = slice(PASSES * P * i0, PASSES * P * i1)
            nc.vector.quantize_mx(
                out=codes[w][:, cols].bitcast(FP8X4), scales=planes[w][:, cols],
                in_=rounded[w][:, i0:i1].rearrange("p t a m j -> p (t a m j)"),
            )

        def g_half(i, u):
            acc = product(3, i, u)
            col = HALVES * i + u
            nc.vector.tensor_scalar(
                g[i][:, BANK * u : BANK * (u + 1)], acc[:], 1.0, None, ALU.mult, ALU.max,
                accum_out=gmax[:, col : col + 1],
            )

        def g_look(i, pieces):
            col = HALVES * i
            nc.vector.tensor_scalar(
                gbias[:, i : i + 1], gmax[:, col : col + 1], gmax[:, col + 1 : col + 2], ntemp[:, i : i + 1],
                ALU.max, ALU.mult,
            )
            for m0, m1 in pieces:
                nc.scalar.activation(
                    c_look[i][:, m0:m1], g[i][:].indirect(pos2_sb[:, m0 // LIST_ROWS : m1 // LIST_ROWS]), ACT.Exp,
                    bias=gbias[:, i : i + 1], scale=temp_sb[:, i : i + 1],
                )

        def left_half(i, u):
            acc = product(1, i, u)
            nc.scalar.copy(left[i][:, BANK * u : BANK * (u + 1)], acc[:])

        def h_half(i, u):
            acc = product(2, i, u)
            cols = slice(BANK * u, BANK * (u + 1))
            nc.vector.tensor_tensor(h[i][:, cols], left[i][:, cols], acc[:], ALU.max)

        def h_look(i):
            nc.vector.tensor_reduce(ntop[:, i : i + 1], h[i][:], AXIS.X, ALU.max, negate=True)
            nc.scalar.activation(a_look[i][:], h[i][:].indirect(pos1_sb[:]), ACT.Exp, bias=ntop[:, i : i + 1])

        def join(i, m0, m1):
            nc.vector.scalar_tensor_tensor(
                prod[:, i, m0:m1], a_look[i][:, m0:m1], lead_sb[:, i : i + 1], c_look[i][:, m0:m1], ALU.mult, ALU.mult
            )

        nc.scalar.copy(
            w1_w[:].rearrange("p (a t c e) -> p a c t e", a=PASSES, t=PACK, e=RUN),
            w1_raw[:].rearrange("p (a c e t) -> p a c t e", a=PASSES, t=PACK, e=RUN),
        )
        round_weight(nc.scalar.copy, 2, 0, 0, 0, SCALAR_SHARE)
        round_weight(nc.vector.tensor_copy, 2, 0, 0, SCALAR_SHARE, P)
        round_weight(nc.vector.tensor_copy, 2, 1, 0, 0, P // 2)
        round_weight(nc.vector.tensor_copy, 2, 1, P // 2, P // 2, P)
        quantize_weight(2, 0, 1)
        quantize_weight(2, 1, 2)
        for u in range(HALVES):
            for i in range(PACK):
                left_half(i, u)
        quantize_weight(2, 2, PACK)
        for a in range(PASSES):
            round_weight(nc.scalar.copy, 3, a, 0, 0, P)

        h_half(0, 0)
        for i in range(LAST - 1):
            h_half(i, 1)
            h_half(i + 1, 0)
            h_look(i)
        h_half(LAST - 1, 1)
        quantize_weight(3, 0, 2)
        h_look(LAST - 1)
        h_half(LAST, 0)
        h_half(LAST, 1)
        quantize_weight(3, 2, PACK)
        nc.vector.tensor_scalar(ntemp[:], temp_sb[:], -1.0, None, ALU.mult)
        h_look(LAST)

        g_half(0, 0)
        for i in range(LAST):
            g_half(i, 1)
            g_half(i + 1, 0)
            g_look(i, [(0, PAIRS)])
        g_half(LAST, 1)
        join(0, 0, PAIRS)
        g_look(LAST, [(0, MH), (MH, PAIRS)])
        for i in range(1, LAST):
            join(i, 0, PAIRS)

        out_view = out.rearrange("(b p) m -> p b m", p=P)

        def round_x(m0, m1):
            x_bf = held([P, (m1 - m0) * PACK], BF16, f"x_bf{m0}")
            nc.vector.tensor_tensor(
                x_bf[:].rearrange("p (c e i) -> p c i e", e=RUN, i=PACK),
                prod[:, :, m0:m1].rearrange("p i (c e) -> p c i e", e=RUN),
                tray_sb[:, :, m0:m1].rearrange("p i (c e) -> p c i e", e=RUN),
                ALU.add,
            )
            return x_bf

        def last_product(x_bf, m0, m1, copies):
            width = m1 - m0
            x_w = held([P, width], U32, f"x_w{m0}")
            x_s = held([P, width], U8, f"x_s{m0}")
            nc.vector.quantize_mx(out=x_w[:].bitcast(FP8X4), scales=x_s[:], in_=x_bf[:])
            per_bank = N // P // len(copies)
            for b, copy in enumerate(copies):
                acc = psum.tile([P, BANK], F32, name="acc")
                for place in range(per_bank):
                    cols = slice(P * (per_bank * b + place), P * (per_bank * b + place + 1))
                    nc.tensor.matmul_mx(
                        out=acc[:, width * place : width * (place + 1)], lhsT=w4_w[:, cols].bitcast(FP8X4),
                        lhsT_scale=w4_s[:, cols], rhs=x_w[:].bitcast(FP8X4), rhs_scale=x_s[:], start=True, stop=True,
                    )
                res = held([P, per_bank * width], F32, f"res{m0}{b}")
                copy(res[:], acc[:, 0 : per_bank * width])
                nc.sync.dma_start(
                    out=out_view[:, per_bank * b : per_bank * (b + 1), m0:m1],
                    in_=res[:].rearrange("p (b m) -> p b m", b=per_bank),
                )

        quarter = MH + MH // 2
        join(LAST, 0, MH)
        x0 = round_x(0, MH)
        join(LAST, MH, PAIRS)
        last_product(x0, 0, MH, (nc.scalar.copy, nc.scalar.copy))
        x1 = round_x(MH, quarter)
        x2 = round_x(quarter, PAIRS)
        last_product(x1, MH, quarter, (nc.vector.tensor_copy,))
        last_product(x2, quarter, PAIRS, (nc.scalar.copy, nc.vector.tensor_copy))
